import numpy as np
import ml_dtypes


def mxq(x, axis, fmt="e4m3"):
    dtype, down = {"e4m3": (ml_dtypes.float8_e4m3fn, 7), "e5m2": (ml_dtypes.float8_e5m2, 14)}[fmt]
    v = np.moveaxis(np.asarray(x, np.float32).astype(ml_dtypes.bfloat16).astype(np.float64), axis, -1)
    blocks = v.reshape(v.shape[:-1] + (-1, 32))
    amax = np.abs(blocks).max(-1, keepdims=True)
    byte = np.maximum(np.where(amax > 0, np.frexp(amax)[1] - 1 + 127, 0) - down, 1)
    scale = np.exp2(byte - 127.0)
    codes = (blocks / scale).astype(np.float32).astype(dtype).astype(np.float64)
    return np.moveaxis((codes * scale).reshape(v.shape), -1, axis)


WIDE = False


def mx_kscale(k):
    if not WIDE:
        return np.ones(k)
    levels = np.array([10, -10, 5, -5, 0])
    if k % 512:
        return np.exp2(np.random.permutation(np.resize(levels, k // 32))).repeat(32)
    a = np.empty((k // 512, 16))
    for p in range(k // 512):
        a[p, :8] = np.random.permutation(np.resize(levels, 8))
        for g in range(8):
            far = levels[np.abs(levels - a[p, g]) >= 10]
            a[p, g + 8] = far[np.random.randint(len(far))]
    return np.exp2(a.ravel()).repeat(32)


def f64(x):
    return np.asarray(x).astype(np.float64)


def striped8(idx):
    return np.asarray(idx).reshape(8, -1, 16).transpose(0, 2, 1).reshape(128, -1).astype(np.uint16)


def unstriped8(offs):
    return offs.reshape(8, 16, -1).transpose(0, 2, 1).reshape(8, -1).astype(np.int64)


def pick8(x, idx, run):
    r = np.arange(len(x))
    return x[r[:, None], idx[r % (8 * run) // run]]


E2M1 = np.array([0.0, 0.5, 1.0, 1.5, 2.0, 3.0, 4.0, 6.0, -0.0, -0.5, -1.0, -1.5, -2.0, -3.0, -4.0, -6.0])


def pack_weight(w, fmt):
    k, n = w.shape
    w = f64(np.asarray(w, np.float32).astype(ml_dtypes.bfloat16)).reshape(k // 32, 32, n)
    amax = np.abs(w).max(1)
    if fmt == "e4m3":
        byte = np.frexp(amax)[1] - 1 + 127 - 7
    else:
        mant, ex = np.frexp(amax / 6.0)
        byte = np.where(mant > 0.5, ex, ex - 1) + 127
    byte = np.clip(np.where(amax > 0, byte, 1), 1, 254)
    scaled = (w * np.exp2(127.0 - byte)[:, None, :]).reshape(k, n).astype(np.float32)
    by_word = np.ascontiguousarray(scaled.reshape(k // 512, 128, 4, n).transpose(0, 1, 3, 2))
    if fmt == "e4m3":
        words = by_word.astype(ml_dtypes.float8_e4m3fn).view(np.uint8)
    else:
        c = by_word.astype(ml_dtypes.float4_e2m1fn).view(np.uint8) & 0xF
        words = (c[..., 0::2] | (c[..., 1::2] << 4)).reshape(k // 512, 128, 2 * n)
    return np.ascontiguousarray(words), np.ascontiguousarray(byte.astype(np.uint8).reshape(k // 512, 16, n))


def unpack_weight(words, scales, fmt):
    g, _, n = scales.shape
    words = np.ascontiguousarray(words).reshape(g, 128, n, -1)
    if fmt == "e4m3":
        vals = words.view(ml_dtypes.float8_e4m3fn).astype(np.float64)
    else:
        nib = np.empty((g, 128, n, 4), np.uint8)
        nib[..., 0::2] = words & 0xF
        nib[..., 1::2] = words >> 4
        vals = E2M1[nib]
    vals = vals * np.repeat(np.exp2(scales.astype(np.float64) - 127.0), 8, axis=1)[..., None]
    return vals.transpose(0, 1, 3, 2).reshape(g * 512, n)


D, K, T, U, I, Q = 512, 512, 1024, 1024, 512, 128


def setup_inputs():
    n = np.random.standard_normal
    idx = np.stack([np.random.permutation(T)[:I] for _ in range(8)])
    idx2 = np.stack([np.random.permutation(U)[:I] for _ in range(8)])
    idx3 = np.stack([np.random.permutation(T)[:I] for _ in range(8)])
    fd = mx_kscale(D)
    fk = mx_kscale(K)
    wqp = pack_weight(n((D, K)) * 1.0 / np.sqrt(D) * fd[:, None] * fk, "e4m3")
    keysp = pack_weight(n((K, T)) * 1.0 / np.sqrt(K) / fk[:, None], "e2m1")
    notesp = pack_weight(n((D, U)) * 1.0 / np.sqrt(D) * fd[:, None], "e4m3")
    return {
        "states": (n((D, Q)) * 0.95 / fd[:, None]).astype(np.float32),
        "wq_words": wqp[0],
        "wq_scales": wqp[1],
        "keys_words": keysp[0],
        "keys_scales": keysp[1],
        "notes_words": notesp[0],
        "notes_scales": notesp[1],
        "offs": striped8(idx),
        "offs2": striped8(idx2),
        "offs3": striped8(idx3),
    }


def reference(states, wq_words, wq_scales, keys_words, keys_scales, notes_words, notes_scales, offs, offs2, offs3):
    idx = unstriped8(offs)
    idx2 = unstriped8(offs2)
    idx3 = unstriped8(offs3)
    wqu = unpack_weight(wq_words, wq_scales, "e4m3")
    keysu = unpack_weight(keys_words, keys_scales, "e2m1")
    notesu = unpack_weight(notes_words, notes_scales, "e4m3")
    statesq = mxq(f64(states), 0, "e4m3")
    qv = wqu.T @ statesq
    qvq = mxq(qv, 0, "e4m3")
    a = qvq.T @ keysu
    b = statesq.T @ notesu
    w = np.maximum(pick8(a, idx, 16), pick8(b, idx2, 16))
    r = w - pick8(a, idx, 16)
    f1 = np.zeros((Q, T))
    f1[np.arange(Q)[:, None], idx[np.arange(Q) % 128 // 16]] = r
    a2 = a + f1
    y = pick8(a2, idx3, 16) - w
    return y

@@ -1,0 +1,163 @@
+from contextlib import ExitStack
+
+import concourse.mybir as mybir
+
+D, K, T, U, I, Q = 512, 512, 1024, 1024, 512, 128
+FLOPS = 2 * (D * K * Q + K * T * Q + D * U * Q)
+
+F32 = mybir.dt.float32
+BF16 = mybir.dt.bfloat16
+I32 = mybir.dt.int32
+U32 = mybir.dt.uint32
+U16 = mybir.dt.uint16
+U8 = mybir.dt.uint8
+FP8X4 = mybir.dt.float8_e4m3fn_x4
+FP4X4 = mybir.dt.float4_e2m1fn_x4
+ALU = mybir.AluOpType
+COPY = mybir.ActivationFunctionType.Copy
+
+P = 128
+PACK = 4
+HALF = I // 2
+HALF_COLS = HALF // 16
+A_TILE = 256
+B_TILE = 512
+CAST_SPLIT = 96
+
+
+def load_scale_rows(queue, plane, scales, rows=range(4)):
+    for r in rows:
+        queue.dma_start(out=plane[r:P:32, :].bitcast(I32), in_=scales[0, r:16:4, :].bitcast(I32))
+
+
+def tile_attend_keptbest_madeside_kernel(
+    tc, states, wq_words, wq_scales, keys_words, keys_scales, notes_words, notes_scales, offs, offs2, offs3, out
+):
+    nc = tc.nc
+    with ExitStack() as ctx:
+        sb = ctx.enter_context(tc.tile_pool(name="sb", bufs=1))
+        ps = ctx.enter_context(tc.psum_pool(name="ps", bufs=1))
+
+        idx_a = sb.tile([P, I // 16], U16, name="idx_a")
+        idx_b = sb.tile([P, I // 16], U16, name="idx_b")
+        idx_o = sb.tile([P, I // 16], U16, name="idx_o")
+
+        st_raw = sb.tile([P, PACK, Q], F32, align_bytes=64)
+        wq_raw = sb.tile([P, K], U32, align_bytes=64)
+        wq_sraw = sb.tile([P, K], U8, align_bytes=64)
+        notes_w = sb.tile([P, U], U32, align_bytes=64)
+        notes_s = sb.tile([P, U], U8, align_bytes=64)
+        keys_w = sb.tile([P, 2 * T], U8, align_bytes=64)
+        keys_s = sb.tile([P, T], U8, align_bytes=64)
+        f1 = sb.tile([P, T], F32, align_bytes=64)
+
+        nc.vector.memset(wq_sraw[:].bitcast(I32), 0)
+        nc.vector.memset(f1[:], 0.0)
+
+        nc.sync.dma_start(out=st_raw[:], in_=states.rearrange("(p j) q -> p j q", j=PACK))
+        load_scale_rows(nc.sync, wq_sraw, wq_scales)
+        nc.sync.dma_start(out=wq_raw[:].bitcast(I32), in_=wq_words[0].rearrange("p n t -> p (n t)").bitcast(I32))
+        nc.sync.dma_start(out=notes_w[:].bitcast(I32), in_=notes_words[0].rearrange("p n t -> p (n t)").bitcast(I32))
+        nc.sync.dma_start(out=keys_w[:].bitcast(I32), in_=keys_words[0].bitcast(I32))
+        load_scale_rows(nc.sync, notes_s, notes_scales)
+        load_scale_rows(nc.sync, keys_s, keys_scales, range(2))
+        nc.sync.dma_start(idx_b[:], offs2)
+        nc.sync.dma_start(idx_a[:], offs)
+        nc.sync.dma_start(idx_o[:], offs3)
+        load_scale_rows(nc.gpsimd, keys_s, keys_scales, range(2, 4))
+
+        wq_s = sb.tile([P, K], U8, align_bytes=64)
+        nc.vector.tensor_copy(
+            out=wq_s[:].rearrange("p (t m) -> p m t", t=PACK), in_=wq_sraw[:].rearrange("p (m t) -> p m t", t=PACK)
+        )
+
+        st_bf = sb.tile([P, Q, PACK], BF16, align_bytes=64)
+        st_view = st_raw[:].rearrange("p j q -> p q j")
+        nc.vector.tensor_copy(out=st_bf[:, :CAST_SPLIT, :], in_=st_view[:, :CAST_SPLIT, :])
+        nc.scalar.activation(st_bf[:, CAST_SPLIT:, :], st_view[:, CAST_SPLIT:, :], COPY)
+        st_c = sb.tile([P, Q], U32, align_bytes=64)
+        st_s = sb.tile([P, Q], U8, align_bytes=64)
+        nc.vector.quantize_mx(out=st_c[:].bitcast(FP8X4), scales=st_s[:], in_=st_bf[:].rearrange("p q j -> p (q j)"))
+
+        wq_lo = sb.tile([P, 2, P], U32, align_bytes=64)
+        wq_hi = sb.tile([P, 2, P], U32, align_bytes=64)
+        wq_view = wq_raw[:].rearrange("p (m t) -> p m t", t=PACK)
+        nc.vector.tensor_copy(out=wq_lo[:].rearrange("p t m -> p m t"), in_=wq_view[:, :, 0:2])
+        nc.scalar.copy(out=wq_hi[:].rearrange("p t m -> p m t"), in_=wq_view[:, :, 2:4])
+
+        qv_ps = ps.tile([P, PACK, Q], F32, name="qv_ps")
+        for t in range(PACK):
+            src = wq_lo if t < 2 else wq_hi
+            nc.tensor.matmul_mx(
+                out=qv_ps[:, t, :],
+                lhsT=src[:, t % 2, :].bitcast(FP8X4),
+                lhsT_scale=wq_s[:, t * P : (t + 1) * P],
+                rhs=st_c[:].bitcast(FP8X4),
+                rhs_scale=st_s[:],
+                start=True,
+                stop=True,
+            )
+        qv_bf = sb.tile([P, Q, PACK], BF16, align_bytes=64)
+        nc.vector.tensor_copy(out=qv_bf[:], in_=qv_ps[:].rearrange("p t q -> p q t"))
+        qv_c = sb.tile([P, Q], U32, align_bytes=64)
+        qv_s = sb.tile([P, Q], U8, align_bytes=64)
+        nc.vector.quantize_mx(out=qv_c[:].bitcast(FP8X4), scales=qv_s[:], in_=qv_bf[:].rearrange("p q j -> p (q j)"))
+
+        b_sb = sb.tile([P, U], F32, align_bytes=64)
+        for j in range(U // B_TILE):
+            cols = slice(j * B_TILE, (j + 1) * B_TILE)
+            b_ps = ps.tile([P, B_TILE], F32, name="b_ps%d" % j)
+            nc.tensor.matmul_mx(
+                out=b_ps[:],
+                lhsT=st_c[:].bitcast(FP8X4),
+                lhsT_scale=st_s[:],
+                rhs=notes_w[:, cols].bitcast(FP8X4),
+                rhs_scale=notes_s[:, cols],
+                start=True,
+                stop=True,
+            )
+            nc.scalar.copy(out=b_sb[:, cols], in_=b_ps[:])
+
+        lo_list = slice(0, HALF_COLS)
+        hi_list = slice(HALF_COLS, 2 * HALF_COLS)
+        gb_lo = sb.tile([P, HALF], F32, align_bytes=64)
+        gb_hi = sb.tile([P, HALF], F32, align_bytes=64)
+        nc.scalar.activation(gb_lo[:], b_sb[:].indirect(idx_b[:, lo_list]), COPY)
+        nc.scalar.activation(gb_hi[:], b_sb[:].indirect(idx_b[:, hi_list]), COPY)
+
+        a_sb = sb.tile([P, T], F32, align_bytes=64)
+        for j in range(T // A_TILE):
+            cols = slice(j * A_TILE, (j + 1) * A_TILE)
+            a_ps = ps.tile([P, A_TILE], F32, name="a_ps%d" % j)
+            nc.tensor.matmul_mx(
+                out=a_ps[:],
+                lhsT=qv_c[:].bitcast(FP8X4),
+                lhsT_scale=qv_s[:],
+                rhs=keys_w[:, 2 * j * A_TILE : 2 * (j + 1) * A_TILE].bitcast(FP4X4),
+                rhs_scale=keys_s[:, cols],
+                start=True,
+                stop=True,
+            )
+            nc.vector.tensor_copy(out=a_sb[:, cols], in_=a_ps[:])
+
+        na_lo = sb.tile([P, HALF], F32, align_bytes=64)
+        na_hi = sb.tile([P, HALF], F32, align_bytes=64)
+        w_lo = sb.tile([P, HALF], F32, align_bytes=64)
+        w_hi = sb.tile([P, HALF], F32, align_bytes=64)
+        nc.vector.tensor_scalar(na_lo[:], a_sb[:].indirect(idx_a[:, lo_list]), -1.0, 0.0, ALU.mult, ALU.add)
+        nc.scalar.activation(na_hi[:], a_sb[:].indirect(idx_a[:, hi_list]), COPY, scale=-1.0)
+        for na, gb, w, lst in ((na_lo, gb_lo, w_lo, lo_list), (na_hi, gb_hi, w_hi, hi_list)):
+            nc.vector.scalar_tensor_tensor(w[:], na[:], -1.0, gb[:], ALU.mult, ALU.max)
+            nc.vector.tensor_tensor(f1[:].indirect(idx_a[:, lst]), w[:], na[:], ALU.add)
+
+        a2 = sb.tile([P, T], F32, align_bytes=64)
+        nc.vector.tensor_tensor(a2[:], a_sb[:], f1[:], ALU.add)
+
+        out_lo = sb.tile([P, HALF], F32, align_bytes=64)
+        out_hi = sb.tile([P, HALF], F32, align_bytes=64)
+        g_hi = sb.tile([P, HALF], F32, align_bytes=64)
+        nc.scalar.activation(g_hi[:], a2[:].indirect(idx_o[:, hi_list]), COPY)
+        nc.vector.tensor_tensor(out_lo[:], a2[:].indirect(idx_o[:, lo_list]), w_lo[:], ALU.subtract)
+        nc.sync.dma_start(out=out[:, :HALF], in_=out_lo[:])
+        nc.vector.tensor_tensor(out_hi[:], g_hi[:], w_hi[:], ALU.subtract)
+        nc.sync.dma_start(out=out[:, HALF:], in_=out_hi[:])

@@ -21,7 +21,7 @@ PACK = 4
 HALF = I // 2
 HALF_COLS = HALF // 16
 A_TILE = 256
-B_TILE = 512
+B_TILE = 256
 CAST_SPLIT = 96
 
 
@@ -58,40 +58,42 @@ def tile_attend_keptbest_madeside_kernel(
         load_scale_rows(nc.sync, wq_sraw, wq_scales)
         nc.sync.dma_start(out=wq_raw[:].bitcast(I32), in_=wq_words[0].rearrange("p n t -> p (n t)").bitcast(I32))
         nc.sync.dma_start(out=notes_w[:].bitcast(I32), in_=notes_words[0].rearrange("p n t -> p (n t)").bitcast(I32))
-        nc.sync.dma_start(out=keys_w[:].bitcast(I32), in_=keys_words[0].bitcast(I32))
         load_scale_rows(nc.sync, notes_s, notes_scales)
         load_scale_rows(nc.sync, keys_s, keys_scales, range(2))
+        nc.sync.dma_start(out=keys_w[:].bitcast(I32), in_=keys_words[0].bitcast(I32))
         nc.sync.dma_start(idx_b[:], offs2)
         nc.sync.dma_start(idx_a[:], offs)
         nc.sync.dma_start(idx_o[:], offs3)
         load_scale_rows(nc.gpsimd, keys_s, keys_scales, range(2, 4))
 
-        wq_s = sb.tile([P, K], U8, align_bytes=64)
-        nc.vector.tensor_copy(
-            out=wq_s[:].rearrange("p (t m) -> p m t", t=PACK), in_=wq_sraw[:].rearrange("p (m t) -> p m t", t=PACK)
-        )
-
         st_bf = sb.tile([P, Q, PACK], BF16, align_bytes=64)
         st_view = st_raw[:].rearrange("p j q -> p q j")
         nc.vector.tensor_copy(out=st_bf[:, :CAST_SPLIT, :], in_=st_view[:, :CAST_SPLIT, :])
         nc.scalar.activation(st_bf[:, CAST_SPLIT:, :], st_view[:, CAST_SPLIT:, :], COPY)
+
+        wq_w = [sb.tile([P, 2, P], U32, align_bytes=64, name="wq_w%d" % h) for h in range(2)]
+        wq_s = [sb.tile([P, 2, P], U8, align_bytes=64, name="wq_s%d" % h) for h in range(2)]
+        words_view = wq_raw[:].rearrange("p (m t) -> p m t", t=PACK)
+        bytes_view = wq_sraw[:].rearrange("p (m t) -> p m t", t=PACK)
+
+        def deal(h):
+            places = slice(2 * h, 2 * h + 2)
+            nc.vector.tensor_copy(out=wq_s[h][:].rearrange("p t m -> p m t"), in_=bytes_view[:, :, places])
+            copy = nc.vector.tensor_copy if h == 0 else nc.scalar.copy
+            copy(out=wq_w[h][:].rearrange("p t m -> p m t"), in_=words_view[:, :, places])
+
+        deal(0)
         st_c = sb.tile([P, Q], U32, align_bytes=64)
         st_s = sb.tile([P, Q], U8, align_bytes=64)
         nc.vector.quantize_mx(out=st_c[:].bitcast(FP8X4), scales=st_s[:], in_=st_bf[:].rearrange("p q j -> p (q j)"))
+        deal(1)
 
-        wq_lo = sb.tile([P, 2, P], U32, align_bytes=64)
-        wq_hi = sb.tile([P, 2, P], U32, align_bytes=64)
-        wq_view = wq_raw[:].rearrange("p (m t) -> p m t", t=PACK)
-        nc.vector.tensor_copy(out=wq_lo[:].rearrange("p t m -> p m t"), in_=wq_view[:, :, 0:2])
-        nc.scalar.copy(out=wq_hi[:].rearrange("p t m -> p m t"), in_=wq_view[:, :, 2:4])
-
-        qv_ps = ps.tile([P, PACK, Q], F32, name="qv_ps")
+        qv_ps = ps.tile([P, PACK, Q], F32, name="qv_ps", tag="a_ps0")
         for t in range(PACK):
-            src = wq_lo if t < 2 else wq_hi
             nc.tensor.matmul_mx(
                 out=qv_ps[:, t, :],
-                lhsT=src[:, t % 2, :].bitcast(FP8X4),
-                lhsT_scale=wq_s[:, t * P : (t + 1) * P],
+                lhsT=wq_w[t // 2][:, t % 2, :].bitcast(FP8X4),
+                lhsT_scale=wq_s[t // 2][:, t % 2, :],
                 rhs=st_c[:].bitcast(FP8X4),
                 rhs_scale=st_s[:],
                 start=True,
@@ -116,19 +118,19 @@ def tile_attend_keptbest_madeside_kernel(
                 start=True,
                 stop=True,
             )
-            nc.scalar.copy(out=b_sb[:, cols], in_=b_ps[:])
+            copy = nc.vector.tensor_copy if j == 1 else nc.scalar.copy
+            copy(out=b_sb[:, cols], in_=b_ps[:])
 
         lo_list = slice(0, HALF_COLS)
         hi_list = slice(HALF_COLS, 2 * HALF_COLS)
-        gb_lo = sb.tile([P, HALF], F32, align_bytes=64)
-        gb_hi = sb.tile([P, HALF], F32, align_bytes=64)
-        nc.scalar.activation(gb_lo[:], b_sb[:].indirect(idx_b[:, lo_list]), COPY)
-        nc.scalar.activation(gb_hi[:], b_sb[:].indirect(idx_b[:, hi_list]), COPY)
+        gb = sb.tile([P, I], F32, align_bytes=64)
+        nc.scalar.activation(gb[:, :HALF], b_sb[:].indirect(idx_b[:, lo_list]), COPY)
+        nc.scalar.activation(gb[:, HALF:], b_sb[:].indirect(idx_b[:, hi_list]), COPY)
 
         a_sb = sb.tile([P, T], F32, align_bytes=64)
         for j in range(T // A_TILE):
             cols = slice(j * A_TILE, (j + 1) * A_TILE)
-            a_ps = ps.tile([P, A_TILE], F32, name="a_ps%d" % j)
+            a_ps = ps.tile([P, A_TILE], F32, name="a_ps%d" % j, tag="a_ps%d" % j)
             nc.tensor.matmul_mx(
                 out=a_ps[:],
                 lhsT=qv_c[:].bitcast(FP8X4),
@@ -140,15 +142,13 @@ def tile_attend_keptbest_madeside_kernel(
             )
             nc.vector.tensor_copy(out=a_sb[:, cols], in_=a_ps[:])
 
-        na_lo = sb.tile([P, HALF], F32, align_bytes=64)
-        na_hi = sb.tile([P, HALF], F32, align_bytes=64)
-        w_lo = sb.tile([P, HALF], F32, align_bytes=64)
-        w_hi = sb.tile([P, HALF], F32, align_bytes=64)
-        nc.vector.tensor_scalar(na_lo[:], a_sb[:].indirect(idx_a[:, lo_list]), -1.0, 0.0, ALU.mult, ALU.add)
-        nc.scalar.activation(na_hi[:], a_sb[:].indirect(idx_a[:, hi_list]), COPY, scale=-1.0)
-        for na, gb, w, lst in ((na_lo, gb_lo, w_lo, lo_list), (na_hi, gb_hi, w_hi, hi_list)):
-            nc.vector.scalar_tensor_tensor(w[:], na[:], -1.0, gb[:], ALU.mult, ALU.max)
-            nc.vector.tensor_tensor(f1[:].indirect(idx_a[:, lst]), w[:], na[:], ALU.add)
+        na = sb.tile([P, I], F32, align_bytes=64)
+        w = sb.tile([P, I], F32, align_bytes=64)
+        nc.vector.tensor_scalar(na[:, :HALF], a_sb[:].indirect(idx_a[:, lo_list]), -1.0, 0.0, ALU.mult, ALU.add)
+        nc.scalar.activation(na[:, HALF:], a_sb[:].indirect(idx_a[:, hi_list]), COPY, scale=-1.0)
+        for half in (slice(0, HALF), slice(HALF, I)):
+            nc.vector.scalar_tensor_tensor(w[:, half], na[:, half], -1.0, gb[:, half], ALU.mult, ALU.max)
+        nc.vector.tensor_tensor(f1[:].indirect(idx_a[:]), w[:], na[:], ALU.add)
 
         a2 = sb.tile([P, T], F32, align_bytes=64)
         nc.vector.tensor_tensor(a2[:], a_sb[:], f1[:], ALU.add)
@@ -157,7 +157,7 @@ def tile_attend_keptbest_madeside_kernel(
         out_hi = sb.tile([P, HALF], F32, align_bytes=64)
         g_hi = sb.tile([P, HALF], F32, align_bytes=64)
         nc.scalar.activation(g_hi[:], a2[:].indirect(idx_o[:, hi_list]), COPY)
-        nc.vector.tensor_tensor(out_lo[:], a2[:].indirect(idx_o[:, lo_list]), w_lo[:], ALU.subtract)
+        nc.vector.tensor_tensor(out_lo[:], a2[:].indirect(idx_o[:, lo_list]), w[:, :HALF], ALU.subtract)
         nc.sync.dma_start(out=out[:, :HALF], in_=out_lo[:])
-        nc.vector.tensor_tensor(out_hi[:], g_hi[:], w_hi[:], ALU.subtract)
+        nc.vector.tensor_tensor(out_hi[:], g_hi[:], w[:, HALF:], ALU.subtract)
         nc.sync.dma_start(out=out[:, HALF:], in_=out_hi[:])

@@ -22,7 +22,6 @@ HALF = I // 2
 HALF_COLS = HALF // 16
 A_TILE = 256
 B_TILE = 256
-CAST_SPLIT = 96
 
 
 def load_scale_rows(queue, plane, scales, rows=range(4)):
@@ -55,21 +54,22 @@ def tile_attend_keptbest_madeside_kernel(
         nc.vector.memset(f1[:], 0.0)
 
         nc.sync.dma_start(out=st_raw[:], in_=states.rearrange("(p j) q -> p j q", j=PACK))
-        load_scale_rows(nc.sync, wq_sraw, wq_scales)
+        load_scale_rows(nc.sync, wq_sraw, wq_scales, range(2))
+        load_scale_rows(nc.scalar, wq_sraw, wq_scales, range(2, 4))
         nc.sync.dma_start(out=wq_raw[:].bitcast(I32), in_=wq_words[0].rearrange("p n t -> p (n t)").bitcast(I32))
         nc.sync.dma_start(out=notes_w[:].bitcast(I32), in_=notes_words[0].rearrange("p n t -> p (n t)").bitcast(I32))
-        load_scale_rows(nc.sync, notes_s, notes_scales)
-        load_scale_rows(nc.sync, keys_s, keys_scales, range(2))
+        load_scale_rows(nc.scalar, notes_s, notes_scales, range(1))
+        load_scale_rows(nc.sync, notes_s, notes_scales, range(1, 4))
         nc.sync.dma_start(out=keys_w[:].bitcast(I32), in_=keys_words[0].bitcast(I32))
+        load_scale_rows(nc.sync, keys_s, keys_scales, range(3))
         nc.sync.dma_start(idx_b[:], offs2)
         nc.sync.dma_start(idx_a[:], offs)
         nc.sync.dma_start(idx_o[:], offs3)
-        load_scale_rows(nc.gpsimd, keys_s, keys_scales, range(2, 4))
+        load_scale_rows(nc.gpsimd, keys_s, keys_scales, range(3, 4))
 
         st_bf = sb.tile([P, Q, PACK], BF16, align_bytes=64)
         st_view = st_raw[:].rearrange("p j q -> p q j")
-        nc.vector.tensor_copy(out=st_bf[:, :CAST_SPLIT, :], in_=st_view[:, :CAST_SPLIT, :])
-        nc.scalar.activation(st_bf[:, CAST_SPLIT:, :], st_view[:, CAST_SPLIT:, :], COPY)
+        nc.vector.tensor_copy(out=st_bf[:], in_=st_view)
 
         wq_w = [sb.tile([P, 2, P], U32, align_bytes=64, name="wq_w%d" % h) for h in range(2)]
         wq_s = [sb.tile([P, 2, P], U8, align_bytes=64, name="wq_s%d" % h) for h in range(2)]
@@ -79,8 +79,7 @@ def tile_attend_keptbest_madeside_kernel(
         def deal(h):
             places = slice(2 * h, 2 * h + 2)
             nc.vector.tensor_copy(out=wq_s[h][:].rearrange("p t m -> p m t"), in_=bytes_view[:, :, places])
-            copy = nc.vector.tensor_copy if h == 0 else nc.scalar.copy
-            copy(out=wq_w[h][:].rearrange("p t m -> p m t"), in_=words_view[:, :, places])
+            nc.vector.tensor_copy(out=wq_w[h][:].rearrange("p t m -> p m t"), in_=words_view[:, :, places])
 
         deal(0)
         st_c = sb.tile([P, Q], U32, align_bytes=64)
@@ -118,8 +117,10 @@ def tile_attend_keptbest_madeside_kernel(
                 start=True,
                 stop=True,
             )
-            copy = nc.vector.tensor_copy if j == 1 else nc.scalar.copy
-            copy(out=b_sb[:, cols], in_=b_ps[:])
+            if j == 1:
+                nc.vector.tensor_copy(out=b_sb[:, cols], in_=b_ps[:])
+            else:
+                nc.scalar.activation(b_sb[:, cols], b_ps[:], COPY)
 
         lo_list = slice(0, HALF_COLS)
         hi_list = slice(HALF_COLS, 2 * HALF_COLS)
@@ -128,6 +129,7 @@ def tile_attend_keptbest_madeside_kernel(
         nc.scalar.activation(gb[:, HALF:], b_sb[:].indirect(idx_b[:, hi_list]), COPY)
 
         a_sb = sb.tile([P, T], F32, align_bytes=64)
+        a_banks = []
         for j in range(T // A_TILE):
             cols = slice(j * A_TILE, (j + 1) * A_TILE)
             a_ps = ps.tile([P, A_TILE], F32, name="a_ps%d" % j, tag="a_ps%d" % j)
@@ -141,6 +143,7 @@ def tile_attend_keptbest_madeside_kernel(
                 stop=True,
             )
             nc.vector.tensor_copy(out=a_sb[:, cols], in_=a_ps[:])
+            a_banks.append(a_ps)
 
         na = sb.tile([P, I], F32, align_bytes=64)
         w = sb.tile([P, I], F32, align_bytes=64)
@@ -151,7 +154,11 @@ def tile_attend_keptbest_madeside_kernel(
         nc.vector.tensor_tensor(f1[:].indirect(idx_a[:]), w[:], na[:], ALU.add)
 
         a2 = sb.tile([P, T], F32, align_bytes=64)
-        nc.vector.tensor_tensor(a2[:], a_sb[:], f1[:], ALU.add)
+        for j in range(3):
+            cols = slice(j * A_TILE, (j + 1) * A_TILE)
+            nc.vector.tensor_tensor(a2[:, cols], a_banks[j][:], f1[:, cols], ALU.add)
+        cols = slice(3 * A_TILE, T)
+        nc.gpsimd.tensor_tensor(a2[:, cols], a_sb[:, cols], f1[:, cols], ALU.add)
 
         out_lo = sb.tile([P, HALF], F32, align_bytes=64)
         out_hi = sb.tile([P, HALF], F32, align_bytes=64)

@@ -18,6 +18,7 @@ COPY = mybir.ActivationFunctionType.Copy
 
 P = 128
 PACK = 4
+LINE = 4
 HALF = I // 2
 HALF_COLS = HALF // 16
 A_TILE = 256
@@ -68,18 +69,19 @@ def tile_attend_keptbest_madeside_kernel(
         load_scale_rows(nc.gpsimd, keys_s, keys_scales, range(3, 4))
 
         st_bf = sb.tile([P, Q, PACK], BF16, align_bytes=64)
-        st_view = st_raw[:].rearrange("p j q -> p q j")
-        nc.vector.tensor_copy(out=st_bf[:], in_=st_view)
+        nc.vector.tensor_copy(
+            out=st_bf[:].rearrange("p (c i) j -> p c j i", i=LINE), in_=st_raw[:].rearrange("p j (c i) -> p c j i", i=LINE)
+        )
 
         wq_w = [sb.tile([P, 2, P], U32, align_bytes=64, name="wq_w%d" % h) for h in range(2)]
         wq_s = [sb.tile([P, 2, P], U8, align_bytes=64, name="wq_s%d" % h) for h in range(2)]
-        words_view = wq_raw[:].rearrange("p (m t) -> p m t", t=PACK)
-        bytes_view = wq_sraw[:].rearrange("p (m t) -> p m t", t=PACK)
+        words_view = wq_raw[:].rearrange("p (c i t) -> p c t i", i=LINE, t=PACK)
+        bytes_view = wq_sraw[:].rearrange("p (m t) -> p t m", t=PACK)
 
         def deal(h):
             places = slice(2 * h, 2 * h + 2)
-            nc.vector.tensor_copy(out=wq_s[h][:].rearrange("p t m -> p m t"), in_=bytes_view[:, :, places])
-            nc.vector.tensor_copy(out=wq_w[h][:].rearrange("p t m -> p m t"), in_=words_view[:, :, places])
+            nc.vector.tensor_copy(out=wq_s[h][:], in_=bytes_view[:, places, :])
+            nc.vector.tensor_copy(out=wq_w[h][:].rearrange("p t (c i) -> p c t i", i=LINE), in_=words_view[:, :, places, :])
 
         deal(0)
         st_c = sb.tile([P, Q], U32, align_bytes=64)

from contextlib import ExitStack

import concourse.mybir as mybir

D, K, T, U, I, Q = 512, 512, 1024, 1024, 512, 128
FLOPS = 2 * (D * K * Q + K * T * Q + D * U * Q)

F32 = mybir.dt.float32
BF16 = mybir.dt.bfloat16
I32 = mybir.dt.int32
U32 = mybir.dt.uint32
U16 = mybir.dt.uint16
U8 = mybir.dt.uint8
FP8X4 = mybir.dt.float8_e4m3fn_x4
FP4X4 = mybir.dt.float4_e2m1fn_x4
ALU = mybir.AluOpType
COPY = mybir.ActivationFunctionType.Copy

P = 128
PACK = 4
LINE = 4
HALF = I // 2
HALF_COLS = HALF // 16
A_TILE = 256
B_TILE = 256


def load_scale_rows(queue, plane, scales, rows=range(4)):
    for r in rows:
        queue.dma_start(out=plane[r:P:32, :].bitcast(I32), in_=scales[0, r:16:4, :].bitcast(I32))


def tile_attend_keptbest_madeside_kernel(
    tc, states, wq_words, wq_scales, keys_words, keys_scales, notes_words, notes_scales, offs, offs2, offs3, out
):
    nc = tc.nc
    with ExitStack() as ctx:
        sb = ctx.enter_context(tc.tile_pool(name="sb", bufs=1))
        ps = ctx.enter_context(tc.psum_pool(name="ps", bufs=1))

        idx_a = sb.tile([P, I // 16], U16, name="idx_a")
        idx_b = sb.tile([P, I // 16], U16, name="idx_b")
        idx_o = sb.tile([P, I // 16], U16, name="idx_o")

        st_raw = sb.tile([P, PACK, Q], F32, align_bytes=64)
        wq_raw = sb.tile([P, K], U32, align_bytes=64)
        wq_sraw = sb.tile([P, K], U8, align_bytes=64)
        notes_w = sb.tile([P, U], U32, align_bytes=64)
        notes_s = sb.tile([P, U], U8, align_bytes=64)
        keys_w = sb.tile([P, 2 * T], U8, align_bytes=64)
        keys_s = sb.tile([P, T], U8, align_bytes=64)
        f1 = sb.tile([P, T], F32, align_bytes=64)

        nc.vector.memset(wq_sraw[:].bitcast(I32), 0)
        nc.vector.memset(f1[:], 0.0)

        nc.sync.dma_start(out=st_raw[:], in_=states.rearrange("(p j) q -> p j q", j=PACK))
        load_scale_rows(nc.sync, wq_sraw, wq_scales, range(2))
        load_scale_rows(nc.scalar, wq_sraw, wq_scales, range(2, 4))
        nc.sync.dma_start(out=wq_raw[:].bitcast(I32), in_=wq_words[0].rearrange("p n t -> p (n t)").bitcast(I32))
        nc.sync.dma_start(out=notes_w[:].bitcast(I32), in_=notes_words[0].rearrange("p n t -> p (n t)").bitcast(I32))
        load_scale_rows(nc.scalar, notes_s, notes_scales, range(1))
        load_scale_rows(nc.sync, notes_s, notes_scales, range(1, 4))
        nc.sync.dma_start(out=keys_w[:].bitcast(I32), in_=keys_words[0].bitcast(I32))
        load_scale_rows(nc.sync, keys_s, keys_scales, range(3))
        nc.sync.dma_start(idx_b[:], offs2)
        nc.sync.dma_start(idx_a[:], offs)
        nc.sync.dma_start(idx_o[:], offs3)
        load_scale_rows(nc.gpsimd, keys_s, keys_scales, range(3, 4))

        st_bf = sb.tile([P, Q, PACK], BF16, align_bytes=64)
        nc.vector.tensor_copy(
            out=st_bf[:].rearrange("p (c i) j -> p c j i", i=LINE), in_=st_raw[:].rearrange("p j (c i) -> p c j i", i=LINE)
        )

        wq_w = [sb.tile([P, 2, P], U32, align_bytes=64, name="wq_w%d" % h) for h in range(2)]
        wq_s = [sb.tile([P, 2, P], U8, align_bytes=64, name="wq_s%d" % h) for h in range(2)]
        words_view = wq_raw[:].rearrange("p (c i t) -> p c t i", i=LINE, t=PACK)
        bytes_view = wq_sraw[:].rearrange("p (m t) -> p t m", t=PACK)

        def deal(h):
            places = slice(2 * h, 2 * h + 2)
            nc.vector.tensor_copy(out=wq_s[h][:], in_=bytes_view[:, places, :])
            nc.vector.tensor_copy(out=wq_w[h][:].rearrange("p t (c i) -> p c t i", i=LINE), in_=words_view[:, :, places, :])

        deal(0)
        st_c = sb.tile([P, Q], U32, align_bytes=64)
        st_s = sb.tile([P, Q], U8, align_bytes=64)
        nc.vector.quantize_mx(out=st_c[:].bitcast(FP8X4), scales=st_s[:], in_=st_bf[:].rearrange("p q j -> p (q j)"))
        deal(1)

        qv_ps = ps.tile([P, PACK, Q], F32, name="qv_ps", tag="a_ps0")
        for t in range(PACK):
            nc.tensor.matmul_mx(
                out=qv_ps[:, t, :],
                lhsT=wq_w[t // 2][:, t % 2, :].bitcast(FP8X4),
                lhsT_scale=wq_s[t // 2][:, t % 2, :],
                rhs=st_c[:].bitcast(FP8X4),
                rhs_scale=st_s[:],
                start=True,
                stop=True,
            )
        qv_bf = sb.tile([P, Q, PACK], BF16, align_bytes=64)
        nc.vector.tensor_copy(out=qv_bf[:], in_=qv_ps[:].rearrange("p t q -> p q t"))
        qv_c = sb.tile([P, Q], U32, align_bytes=64)
        qv_s = sb.tile([P, Q], U8, align_bytes=64)
        nc.vector.quantize_mx(out=qv_c[:].bitcast(FP8X4), scales=qv_s[:], in_=qv_bf[:].rearrange("p q j -> p (q j)"))

        b_sb = sb.tile([P, U], F32, align_bytes=64)
        for j in range(U // B_TILE):
            cols = slice(j * B_TILE, (j + 1) * B_TILE)
            b_ps = ps.tile([P, B_TILE], F32, name="b_ps%d" % j)
            nc.tensor.matmul_mx(
                out=b_ps[:],
                lhsT=st_c[:].bitcast(FP8X4),
                lhsT_scale=st_s[:],
                rhs=notes_w[:, cols].bitcast(FP8X4),
                rhs_scale=notes_s[:, cols],
                start=True,
                stop=True,
            )
            if j == 1:
                nc.vector.tensor_copy(out=b_sb[:, cols], in_=b_ps[:])
            else:
                nc.scalar.activation(b_sb[:, cols], b_ps[:], COPY)

        lo_list = slice(0, HALF_COLS)
        hi_list = slice(HALF_COLS, 2 * HALF_COLS)
        gb = sb.tile([P, I], F32, align_bytes=64)
        nc.scalar.activation(gb[:, :HALF], b_sb[:].indirect(idx_b[:, lo_list]), COPY)
        nc.scalar.activation(gb[:, HALF:], b_sb[:].indirect(idx_b[:, hi_list]), COPY)

        a_sb = sb.tile([P, T], F32, align_bytes=64)
        a_banks = []
        for j in range(T // A_TILE):
            cols = slice(j * A_TILE, (j + 1) * A_TILE)
            a_ps = ps.tile([P, A_TILE], F32, name="a_ps%d" % j, tag="a_ps%d" % j)
            nc.tensor.matmul_mx(
                out=a_ps[:],
                lhsT=qv_c[:].bitcast(FP8X4),
                lhsT_scale=qv_s[:],
                rhs=keys_w[:, 2 * j * A_TILE : 2 * (j + 1) * A_TILE].bitcast(FP4X4),
                rhs_scale=keys_s[:, cols],
                start=True,
                stop=True,
            )
            nc.vector.tensor_copy(out=a_sb[:, cols], in_=a_ps[:])
            a_banks.append(a_ps)

        na = sb.tile([P, I], F32, align_bytes=64)
        w = sb.tile([P, I], F32, align_bytes=64)
        nc.vector.tensor_scalar(na[:, :HALF], a_sb[:].indirect(idx_a[:, lo_list]), -1.0, 0.0, ALU.mult, ALU.add)
        nc.scalar.activation(na[:, HALF:], a_sb[:].indirect(idx_a[:, hi_list]), COPY, scale=-1.0)
        for half in (slice(0, HALF), slice(HALF, I)):
            nc.vector.scalar_tensor_tensor(w[:, half], na[:, half], -1.0, gb[:, half], ALU.mult, ALU.max)
        nc.vector.tensor_tensor(f1[:].indirect(idx_a[:]), w[:], na[:], ALU.add)

        a2 = sb.tile([P, T], F32, align_bytes=64)
        for j in range(3):
            cols = slice(j * A_TILE, (j + 1) * A_TILE)
            nc.vector.tensor_tensor(a2[:, cols], a_banks[j][:], f1[:, cols], ALU.add)
        cols = slice(3 * A_TILE, T)
        nc.gpsimd.tensor_tensor(a2[:, cols], a_sb[:, cols], f1[:, cols], ALU.add)

        out_lo = sb.tile([P, HALF], F32, align_bytes=64)
        out_hi = sb.tile([P, HALF], F32, align_bytes=64)
        g_hi = sb.tile([P, HALF], F32, align_bytes=64)
        nc.scalar.activation(g_hi[:], a2[:].indirect(idx_o[:, hi_list]), COPY)
        nc.vector.tensor_tensor(out_lo[:], a2[:].indirect(idx_o[:, lo_list]), w[:, :HALF], ALU.subtract)
        nc.sync.dma_start(out=out[:, :HALF], in_=out_lo[:])
        nc.vector.tensor_tensor(out_hi[:], g_hi[:], w[:, HALF:], ALU.subtract)
        nc.sync.dma_start(out=out[:, HALF:], in_=out_hi[:])
